import numpy as np
import ml_dtypes

BF16 = ml_dtypes.bfloat16


def bf(x):
    return np.asarray(x, np.float32).astype(BF16)


def f32(x):
    return np.asarray(x, np.float32)


def f64(x):
    return np.asarray(x).astype(np.float64)


def striped(idx):
    return np.tile(idx.reshape(-1, 16).T, (8, 1))


S, K, M, N, E, Q = 512, 128, 512, 256, 4, 64


def setup_inputs():
    return {"base": bf(np.random.standard_normal((M, S))), "x": bf(np.random.standard_normal((K, N))), "w": bf(np.random.standard_normal((E, K, M)) / np.sqrt(K)), "b": f32(0.5 * np.random.standard_normal((M, 1))), "offs": striped(np.random.permutation(S)[:N])}


def reference(base, x, w, b, offs):
    idx = offs[:16].T.reshape(-1)
    z = f64(base).copy()
    for e in range(E):
        z[:, idx[e * Q : (e + 1) * Q]] = f64(w)[e].T @ f64(x)[:, e * Q : (e + 1) * Q]
    return np.maximum(z + f64(b), 0.0)

@@ -1,0 +1,64 @@
+import concourse.mybir as mybir
+from concourse.masks import make_identity
+
+BF16, F32, U16 = mybir.dt.bfloat16, mybir.dt.float32, mybir.dt.uint16
+ADD, MAX = mybir.AluOpType.add, mybir.AluOpType.max
+RELU = mybir.ActivationFunctionType.Relu
+
+P = 128
+TOKENS = 512
+FEATURES = 512
+LISTED = 256
+EXPERTS = 4
+PIECE = LISTED // EXPERTS
+PIECE_COLS = PIECE // 16
+WINDOWS = FEATURES // P
+
+FLOPS = 2 * P * FEATURES * LISTED
+
+
+def tile_scatter_matmul_kernel(tc, base, x, w, b, offs, out):
+    nc = tc.nc
+    with (
+        tc.tile_pool(name="held", bufs=1) as held,
+        tc.psum_pool(name="banks", bufs=1) as banks,
+    ):
+        offsets = held.tile([P, LISTED // 16], U16, name="offsets")
+        nc.sync.dma_start(offsets[:], offs)
+
+        ident = held.tile([P, P], BF16, name="ident")
+        make_identity(nc, ident[:])
+
+        base_blocks = [held.tile([P, TOKENS], BF16, name="base%d" % a) for a in range(WINDOWS)]
+        for a in range(WINDOWS):
+            queue = nc.sync if a % 2 == 0 else nc.scalar
+            queue.dma_start(base_blocks[a][:], base[a * P : (a + 1) * P, :])
+
+        x_tile = held.tile([P, LISTED], BF16, name="x_tile")
+        nc.sync.dma_start(x_tile[:], x)
+        w_tile = held.tile([P, EXPERTS, FEATURES], BF16, name="w_tile")
+        nc.scalar.dma_start(w_tile[:], w.rearrange("e k m -> k e m"))
+
+        bias = held.tile([P, WINDOWS], F32, name="bias")
+        with nc.allow_non_contiguous_dma(reason="one float32 value to a partition"):
+            nc.sync.dma_start(bias[:], b.rearrange("(a p) o -> p (a o)", p=P))
+
+        windows = [banks.tile([P, TOKENS], F32, name="window%d" % a) for a in range(WINDOWS)]
+        for a in range(WINDOWS):
+            nc.tensor.matmul(windows[a][:], ident[:], base_blocks[a][:], start=True, stop=True)
+
+        for a in range(WINDOWS):
+            for e in range(EXPERTS):
+                nc.tensor.matmul(
+                    windows[a][:].indirect(offsets[:, e * PIECE_COLS : (e + 1) * PIECE_COLS]),
+                    w_tile[:, e, a * P : (a + 1) * P],
+                    x_tile[:, e * PIECE : (e + 1) * PIECE],
+                    start=True,
+                    stop=True,
+                )
+            result = held.tile([P, TOKENS], F32, name="result%d" % a)
+            if a % 2 == 0:
+                nc.scalar.activation(result[:], windows[a][:], RELU, bias=bias[:, a : a + 1])
+            else:
+                nc.vector.tensor_scalar(result[:], windows[a][:], bias[:, a : a + 1], 0.0, ADD, MAX)
+            nc.sync.dma_start(out[a * P : (a + 1) * P, :], result[:])

@@ -14,6 +14,8 @@ PIECE = LISTED // EXPERTS
 PIECE_COLS = PIECE // 16
 WINDOWS = FEATURES // P
 
+WARMUPS = 3
+
 FLOPS = 2 * P * FEATURES * LISTED
 
 
@@ -29,6 +31,16 @@ def tile_scatter_matmul_kernel(tc, base, x, w, b, offs, out):
         ident = held.tile([P, P], BF16, name="ident")
         make_identity(nc, ident[:])
 
+        zeros = held.tile([P, TOKENS], BF16, name="zeros")
+        nc.vector.memset(zeros[:], 0.0)
+        unread = banks.tile([P, TOKENS], F32, name="unread")
+        for _ in range(WARMUPS):
+            nc.tensor.matmul(unread[:], zeros[:, 0:P], zeros[:], start=True, stop=True)
+
+        scratch = held.tile([P, 1], F32, name="scratch")
+        nc.vector.memset(scratch[:], 0.0)
+        nc.scalar.activation(scratch[:], scratch[:], RELU)
+
         base_blocks = [held.tile([P, TOKENS], BF16, name="base%d" % a) for a in range(WINDOWS)]
         for a in range(WINDOWS):
             queue = nc.sync if a % 2 == 0 else nc.scalar
@@ -36,8 +48,10 @@ def tile_scatter_matmul_kernel(tc, base, x, w, b, offs, out):
 
         x_tile = held.tile([P, LISTED], BF16, name="x_tile")
         nc.sync.dma_start(x_tile[:], x)
-        w_tile = held.tile([P, EXPERTS, FEATURES], BF16, name="w_tile")
-        nc.scalar.dma_start(w_tile[:], w.rearrange("e k m -> k e m"))
+        w_tiles = [held.tile([P, FEATURES], BF16, name="w%d" % e) for e in range(EXPERTS)]
+        for e in range(EXPERTS):
+            queue = nc.scalar if e % 2 == 0 else nc.sync
+            queue.dma_start(w_tiles[e][:], w[e])
 
         bias = held.tile([P, WINDOWS], F32, name="bias")
         with nc.allow_non_contiguous_dma(reason="one float32 value to a partition"):
@@ -47,18 +61,22 @@ def tile_scatter_matmul_kernel(tc, base, x, w, b, offs, out):
         for a in range(WINDOWS):
             nc.tensor.matmul(windows[a][:], ident[:], base_blocks[a][:], start=True, stop=True)
 
+        def place(e, a):
+            nc.tensor.matmul(
+                windows[a][:].indirect(offsets[:, e * PIECE_COLS : (e + 1) * PIECE_COLS]),
+                w_tiles[e][:, a * P : (a + 1) * P],
+                x_tile[:, e * PIECE : (e + 1) * PIECE],
+                start=True,
+                stop=True,
+            )
+
         for a in range(WINDOWS):
             for e in range(EXPERTS):
-                nc.tensor.matmul(
-                    windows[a][:].indirect(offsets[:, e * PIECE_COLS : (e + 1) * PIECE_COLS]),
-                    w_tile[:, e, a * P : (a + 1) * P],
-                    x_tile[:, e * PIECE : (e + 1) * PIECE],
-                    start=True,
-                    stop=True,
-                )
+                place(e, a)
             result = held.tile([P, TOKENS], F32, name="result%d" % a)
             if a % 2 == 0:
                 nc.scalar.activation(result[:], windows[a][:], RELU, bias=bias[:, a : a + 1])
+                nc.scalar.dma_start(out[a * P : (a + 1) * P, :], result[:])
             else:
                 nc.vector.tensor_scalar(result[:], windows[a][:], bias[:, a : a + 1], 0.0, ADD, MAX)
-            nc.sync.dma_start(out[a * P : (a + 1) * P, :], result[:])
+                nc.sync.dma_start(out[a * P : (a + 1) * P, :], result[:])

@@ -43,15 +43,13 @@ def tile_scatter_matmul_kernel(tc, base, x, w, b, offs, out):
 
         base_blocks = [held.tile([P, TOKENS], BF16, name="base%d" % a) for a in range(WINDOWS)]
         for a in range(WINDOWS):
-            queue = nc.sync if a % 2 == 0 else nc.scalar
-            queue.dma_start(base_blocks[a][:], base[a * P : (a + 1) * P, :])
+            nc.sync.dma_start(base_blocks[a][:], base[a * P : (a + 1) * P, :])
 
         x_tile = held.tile([P, LISTED], BF16, name="x_tile")
         nc.sync.dma_start(x_tile[:], x)
         w_tiles = [held.tile([P, FEATURES], BF16, name="w%d" % e) for e in range(EXPERTS)]
         for e in range(EXPERTS):
-            queue = nc.scalar if e % 2 == 0 else nc.sync
-            queue.dma_start(w_tiles[e][:], w[e])
+            nc.sync.dma_start(w_tiles[e][:], w[e])
 
         bias = held.tile([P, WINDOWS], F32, name="bias")
         with nc.allow_non_contiguous_dma(reason="one float32 value to a partition"):

@@ -15,6 +15,7 @@ PIECE_COLS = PIECE // 16
 WINDOWS = FEATURES // P
 
 WARMUPS = 3
+PADDED = 32
 
 FLOPS = 2 * P * FEATURES * LISTED
 
@@ -25,11 +26,17 @@ def tile_scatter_matmul_kernel(tc, base, x, w, b, offs, out):
         tc.tile_pool(name="held", bufs=1) as held,
         tc.psum_pool(name="banks", bufs=1) as banks,
     ):
+        bias_rows = held.tile([PADDED, P], F32, name="bias_rows")
+        nc.vector.memset(bias_rows[:], 0.0)
+        nc.scalar.dma_start(bias_rows[0:WINDOWS, :], b.rearrange("(a p) o -> a (p o)", p=P))
+
         offsets = held.tile([P, LISTED // 16], U16, name="offsets")
         nc.sync.dma_start(offsets[:], offs)
 
         ident = held.tile([P, P], BF16, name="ident")
         make_identity(nc, ident[:])
+        small_ident = held.tile([PADDED, PADDED], F32, name="small_ident")
+        make_identity(nc, small_ident[:])
 
         zeros = held.tile([P, TOKENS], BF16, name="zeros")
         nc.vector.memset(zeros[:], 0.0)
@@ -51,13 +58,14 @@ def tile_scatter_matmul_kernel(tc, base, x, w, b, offs, out):
         for e in range(EXPERTS):
             nc.sync.dma_start(w_tiles[e][:], w[e])
 
-        bias = held.tile([P, WINDOWS], F32, name="bias")
-        with nc.allow_non_contiguous_dma(reason="one float32 value to a partition"):
-            nc.sync.dma_start(bias[:], b.rearrange("(a p) o -> p (a o)", p=P))
-
         windows = [banks.tile([P, TOKENS], F32, name="window%d" % a) for a in range(WINDOWS)]
         for a in range(WINDOWS):
             nc.tensor.matmul(windows[a][:], ident[:], base_blocks[a][:], start=True, stop=True)
+
+        bias_bank = banks.tile([P, WINDOWS], F32, name="bias_bank")
+        nc.tensor.matmul(bias_bank[:], bias_rows[:], small_ident[:, 0:WINDOWS], start=True, stop=True)
+        bias = held.tile([P, WINDOWS], F32, name="bias")
+        nc.vector.tensor_copy(bias[:], bias_bank[:])
 
         def place(e, a):
             nc.tensor.matmul(

@@ -13,6 +13,7 @@ EXPERTS = 4
 PIECE = LISTED // EXPERTS
 PIECE_COLS = PIECE // 16
 WINDOWS = FEATURES // P
+HALF = FEATURES // 2
 
 WARMUPS = 3
 PADDED = 32
@@ -54,9 +55,11 @@ def tile_scatter_matmul_kernel(tc, base, x, w, b, offs, out):
 
         x_tile = held.tile([P, LISTED], BF16, name="x_tile")
         nc.sync.dma_start(x_tile[:], x)
-        w_tiles = [held.tile([P, FEATURES], BF16, name="w%d" % e) for e in range(EXPERTS)]
-        for e in range(EXPERTS):
-            nc.sync.dma_start(w_tiles[e][:], w[e])
+
+        w_by_k = w.rearrange("e k m -> k e m")
+        w_halves = [held.tile([P, EXPERTS, HALF], BF16, name="w_half%d" % h) for h in range(2)]
+        for h in range(2):
+            nc.sync.dma_start(w_halves[h][:], w_by_k[:, :, h * HALF : (h + 1) * HALF])
 
         windows = [banks.tile([P, TOKENS], F32, name="window%d" % a) for a in range(WINDOWS)]
         for a in range(WINDOWS):
@@ -70,7 +73,7 @@ def tile_scatter_matmul_kernel(tc, base, x, w, b, offs, out):
         def place(e, a):
             nc.tensor.matmul(
                 windows[a][:].indirect(offsets[:, e * PIECE_COLS : (e + 1) * PIECE_COLS]),
-                w_tiles[e][:, a * P : (a + 1) * P],
+                w_halves[a // 2][:, e, (a % 2) * P : (a % 2 + 1) * P],
                 x_tile[:, e * PIECE : (e + 1) * PIECE],
                 start=True,
                 stop=True,

@@ -15,7 +15,7 @@ PIECE_COLS = PIECE // 16
 WINDOWS = FEATURES // P
 HALF = FEATURES // 2
 
-WARMUPS = 3
+WARMUPS = 2
 PADDED = 32
 
 FLOPS = 2 * P * FEATURES * LISTED
@@ -57,9 +57,11 @@ def tile_scatter_matmul_kernel(tc, base, x, w, b, offs, out):
         nc.sync.dma_start(x_tile[:], x)
 
         w_by_k = w.rearrange("e k m -> k e m")
-        w_halves = [held.tile([P, EXPERTS, HALF], BF16, name="w_half%d" % h) for h in range(2)]
+        w_parts = {}
         for h in range(2):
-            nc.sync.dma_start(w_halves[h][:], w_by_k[:, :, h * HALF : (h + 1) * HALF])
+            for q in range(EXPERTS // 2):
+                w_parts[h, q] = held.tile([P, 2, HALF], BF16, name="w_part%d_%d" % (h, q))
+                nc.sync.dma_start(w_parts[h, q][:], w_by_k[:, 2 * q : 2 * q + 2, h * HALF : (h + 1) * HALF])
 
         windows = [banks.tile([P, TOKENS], F32, name="window%d" % a) for a in range(WINDOWS)]
         for a in range(WINDOWS):
@@ -73,7 +75,7 @@ def tile_scatter_matmul_kernel(tc, base, x, w, b, offs, out):
         def place(e, a):
             nc.tensor.matmul(
                 windows[a][:].indirect(offsets[:, e * PIECE_COLS : (e + 1) * PIECE_COLS]),
-                w_halves[a // 2][:, e, (a % 2) * P : (a % 2 + 1) * P],
+                w_parts[a // 2, e // 2][:, e % 2, (a % 2) * P : (a % 2 + 1) * P],
                 x_tile[:, e * PIECE : (e + 1) * PIECE],
                 start=True,
                 stop=True,

@@ -14,6 +14,8 @@ PIECE = LISTED // EXPERTS
 PIECE_COLS = PIECE // 16
 WINDOWS = FEATURES // P
 HALF = FEATURES // 2
+PAIR = 2
+FILL_PIECE = 32
 
 WARMUPS = 2
 PADDED = 32
@@ -50,22 +52,28 @@ def tile_scatter_matmul_kernel(tc, base, x, w, b, offs, out):
         nc.scalar.activation(scratch[:], scratch[:], RELU)
 
         base_blocks = [held.tile([P, TOKENS], BF16, name="base%d" % a) for a in range(WINDOWS)]
-        for a in range(WINDOWS):
-            nc.sync.dma_start(base_blocks[a][:], base[a * P : (a + 1) * P, :])
-
         x_tile = held.tile([P, LISTED], BF16, name="x_tile")
-        nc.sync.dma_start(x_tile[:], x)
-
         w_by_k = w.rearrange("e k m -> k e m")
         w_parts = {}
-        for h in range(2):
+        for h in range(WINDOWS // PAIR):
+            for a in range(h * PAIR, (h + 1) * PAIR):
+                nc.sync.dma_start(base_blocks[a][:], base[a * P : (a + 1) * P, :])
+            if h == 0:
+                nc.sync.dma_start(x_tile[:], x)
             for q in range(EXPERTS // 2):
                 w_parts[h, q] = held.tile([P, 2, HALF], BF16, name="w_part%d_%d" % (h, q))
                 nc.sync.dma_start(w_parts[h, q][:], w_by_k[:, 2 * q : 2 * q + 2, h * HALF : (h + 1) * HALF])
 
         windows = [banks.tile([P, TOKENS], F32, name="window%d" % a) for a in range(WINDOWS)]
-        for a in range(WINDOWS):
-            nc.tensor.matmul(windows[a][:], ident[:], base_blocks[a][:], start=True, stop=True)
+
+        def fill(a, piece):
+            for c in range(0, TOKENS, piece):
+                nc.tensor.matmul(
+                    windows[a][:, c : c + piece], ident[:], base_blocks[a][:, c : c + piece], start=True, stop=True
+                )
+
+        for a in range(PAIR):
+            fill(a, TOKENS)
 
         bias_bank = banks.tile([P, WINDOWS], F32, name="bias_bank")
         nc.tensor.matmul(bias_bank[:], bias_rows[:], small_ident[:, 0:WINDOWS], start=True, stop=True)
@@ -82,6 +90,9 @@ def tile_scatter_matmul_kernel(tc, base, x, w, b, offs, out):
             )
 
         for a in range(WINDOWS):
+            if a == PAIR:
+                for late in range(PAIR, WINDOWS):
+                    fill(late, FILL_PIECE)
             for e in range(EXPERTS):
                 place(e, a)
             result = held.tile([P, TOKENS], F32, name="result%d" % a)

@@ -15,7 +15,7 @@ PIECE_COLS = PIECE // 16
 WINDOWS = FEATURES // P
 HALF = FEATURES // 2
 PAIR = 2
-FILL_PIECE = 32
+FILL_PIECE = 44
 
 WARMUPS = 2
 PADDED = 32
@@ -29,6 +29,9 @@ def tile_scatter_matmul_kernel(tc, base, x, w, b, offs, out):
         tc.tile_pool(name="held", bufs=1) as held,
         tc.psum_pool(name="banks", bufs=1) as banks,
     ):
+        zeros = held.tile([P, TOKENS], BF16, name="zeros")
+        nc.vector.memset(zeros[:], 0.0)
+
         bias_rows = held.tile([PADDED, P], F32, name="bias_rows")
         nc.vector.memset(bias_rows[:], 0.0)
         nc.scalar.dma_start(bias_rows[0:WINDOWS, :], b.rearrange("(a p) o -> a (p o)", p=P))
@@ -41,8 +44,6 @@ def tile_scatter_matmul_kernel(tc, base, x, w, b, offs, out):
         small_ident = held.tile([PADDED, PADDED], F32, name="small_ident")
         make_identity(nc, small_ident[:])
 
-        zeros = held.tile([P, TOKENS], BF16, name="zeros")
-        nc.vector.memset(zeros[:], 0.0)
         unread = banks.tile([P, TOKENS], F32, name="unread")
         for _ in range(WARMUPS):
             nc.tensor.matmul(unread[:], zeros[:, 0:P], zeros[:], start=True, stop=True)
@@ -68,9 +69,8 @@ def tile_scatter_matmul_kernel(tc, base, x, w, b, offs, out):
 
         def fill(a, piece):
             for c in range(0, TOKENS, piece):
-                nc.tensor.matmul(
-                    windows[a][:, c : c + piece], ident[:], base_blocks[a][:, c : c + piece], start=True, stop=True
-                )
+                end = min(c + piece, TOKENS)
+                nc.tensor.matmul(windows[a][:, c:end], ident[:], base_blocks[a][:, c:end], start=True, stop=True)
 
         for a in range(PAIR):
             fill(a, TOKENS)

@@ -18,7 +18,7 @@ PAIR = 2
 FILL_PIECE = 44
 
 WARMUPS = 2
-PADDED = 32
+BLOCK = 32
 
 FLOPS = 2 * P * FEATURES * LISTED
 
@@ -32,17 +32,18 @@ def tile_scatter_matmul_kernel(tc, base, x, w, b, offs, out):
         zeros = held.tile([P, TOKENS], BF16, name="zeros")
         nc.vector.memset(zeros[:], 0.0)
 
-        bias_rows = held.tile([PADDED, P], F32, name="bias_rows")
-        nc.vector.memset(bias_rows[:], 0.0)
-        nc.scalar.dma_start(bias_rows[0:WINDOWS, :], b.rearrange("(a p) o -> a (p o)", p=P))
+        bias_rows = held.tile([P, P], F32, name="bias_rows", align_bytes=64)
+        nc.gpsimd.memset(bias_rows[:], 0.0)
+        nc.scalar.dma_start(
+            bias_rows[0:P:BLOCK, :].rearrange("g (a i) -> g a i", i=BLOCK),
+            b.rearrange("(a g i) o -> g a (i o)", g=P // BLOCK, i=BLOCK),
+        )
 
         offsets = held.tile([P, LISTED // 16], U16, name="offsets")
         nc.sync.dma_start(offsets[:], offs)
 
         ident = held.tile([P, P], BF16, name="ident")
         make_identity(nc, ident[:])
-        small_ident = held.tile([PADDED, PADDED], F32, name="small_ident")
-        make_identity(nc, small_ident[:])
 
         unread = banks.tile([P, TOKENS], F32, name="unread")
         for _ in range(WARMUPS):
@@ -51,6 +52,9 @@ def tile_scatter_matmul_kernel(tc, base, x, w, b, offs, out):
         scratch = held.tile([P, 1], F32, name="scratch")
         nc.vector.memset(scratch[:], 0.0)
         nc.scalar.activation(scratch[:], scratch[:], RELU)
+
+        bias = held.tile([P, P], F32, name="bias", align_bytes=64)
+        nc.vector.transpose(bias[:], bias_rows[:])
 
         base_blocks = [held.tile([P, TOKENS], BF16, name="base%d" % a) for a in range(WINDOWS)]
         x_tile = held.tile([P, LISTED], BF16, name="x_tile")
@@ -75,11 +79,6 @@ def tile_scatter_matmul_kernel(tc, base, x, w, b, offs, out):
         for a in range(PAIR):
             fill(a, TOKENS)
 
-        bias_bank = banks.tile([P, WINDOWS], F32, name="bias_bank")
-        nc.tensor.matmul(bias_bank[:], bias_rows[:], small_ident[:, 0:WINDOWS], start=True, stop=True)
-        bias = held.tile([P, WINDOWS], F32, name="bias")
-        nc.vector.tensor_copy(bias[:], bias_bank[:])
-
         def place(e, a):
             nc.tensor.matmul(
                 windows[a][:].indirect(offsets[:, e * PIECE_COLS : (e + 1) * PIECE_COLS]),
@@ -96,9 +95,10 @@ def tile_scatter_matmul_kernel(tc, base, x, w, b, offs, out):
             for e in range(EXPERTS):
                 place(e, a)
             result = held.tile([P, TOKENS], F32, name="result%d" % a)
+            bias_column = bias[:, a * BLOCK : a * BLOCK + 1]
             if a % 2 == 0:
-                nc.scalar.activation(result[:], windows[a][:], RELU, bias=bias[:, a : a + 1])
+                nc.scalar.activation(result[:], windows[a][:], RELU, bias=bias_column)
                 nc.scalar.dma_start(out[a * P : (a + 1) * P, :], result[:])
             else:
-                nc.vector.tensor_scalar(result[:], windows[a][:], bias[:, a : a + 1], 0.0, ADD, MAX)
+                nc.vector.tensor_scalar(result[:], windows[a][:], bias_column, 0.0, ADD, MAX)
                 nc.sync.dma_start(out[a * P : (a + 1) * P, :], result[:])

@@ -17,7 +17,7 @@ HALF = FEATURES // 2
 PAIR = 2
 FILL_PIECE = 44
 
-WARMUPS = 2
+WARMUPS = 8
 BLOCK = 32
 
 FLOPS = 2 * P * FEATURES * LISTED
@@ -29,7 +29,7 @@ def tile_scatter_matmul_kernel(tc, base, x, w, b, offs, out):
         tc.tile_pool(name="held", bufs=1) as held,
         tc.psum_pool(name="banks", bufs=1) as banks,
     ):
-        zeros = held.tile([P, TOKENS], BF16, name="zeros")
+        zeros = held.tile([P, P], BF16, name="zeros")
         nc.vector.memset(zeros[:], 0.0)
 
         bias_rows = held.tile([P, P], F32, name="bias_rows", align_bytes=64)
@@ -39,15 +39,12 @@ def tile_scatter_matmul_kernel(tc, base, x, w, b, offs, out):
             b.rearrange("(a g i) o -> g a (i o)", g=P // BLOCK, i=BLOCK),
         )
 
-        offsets = held.tile([P, LISTED // 16], U16, name="offsets")
-        nc.sync.dma_start(offsets[:], offs)
-
         ident = held.tile([P, P], BF16, name="ident")
         make_identity(nc, ident[:])
 
-        unread = banks.tile([P, TOKENS], F32, name="unread")
+        unread = banks.tile([P, P], F32, name="unread")
         for _ in range(WARMUPS):
-            nc.tensor.matmul(unread[:], zeros[:, 0:P], zeros[:], start=True, stop=True)
+            nc.tensor.matmul(unread[:], zeros[:], zeros[:], start=True, stop=True)
 
         scratch = held.tile([P, 1], F32, name="scratch")
         nc.vector.memset(scratch[:], 0.0)
@@ -58,12 +55,14 @@ def tile_scatter_matmul_kernel(tc, base, x, w, b, offs, out):
 
         base_blocks = [held.tile([P, TOKENS], BF16, name="base%d" % a) for a in range(WINDOWS)]
         x_tile = held.tile([P, LISTED], BF16, name="x_tile")
+        offsets = held.tile([P, LISTED // 16], U16, name="offsets")
         w_by_k = w.rearrange("e k m -> k e m")
         w_parts = {}
         for h in range(WINDOWS // PAIR):
             for a in range(h * PAIR, (h + 1) * PAIR):
                 nc.sync.dma_start(base_blocks[a][:], base[a * P : (a + 1) * P, :])
             if h == 0:
+                nc.sync.dma_start(offsets[:], offs)
                 nc.sync.dma_start(x_tile[:], x)
             for q in range(EXPERTS // 2):
                 w_parts[h, q] = held.tile([P, 2, HALF], BF16, name="w_part%d_%d" % (h, q))

@@ -87,12 +87,7 @@ def tile_scatter_matmul_kernel(tc, base, x, w, b, offs, out):
                 stop=True,
             )
 
-        for a in range(WINDOWS):
-            if a == PAIR:
-                for late in range(PAIR, WINDOWS):
-                    fill(late, FILL_PIECE)
-            for e in range(EXPERTS):
-                place(e, a)
+        def finish(a):
             result = held.tile([P, TOKENS], F32, name="result%d" % a)
             bias_column = bias[:, a * BLOCK : a * BLOCK + 1]
             if a % 2 == 0:
@@ -101,3 +96,15 @@ def tile_scatter_matmul_kernel(tc, base, x, w, b, offs, out):
             else:
                 nc.vector.tensor_scalar(result[:], windows[a][:], bias_column, 0.0, ADD, MAX)
                 nc.sync.dma_start(out[a * P : (a + 1) * P, :], result[:])
+
+        for h in range(WINDOWS // PAIR):
+            pair = range(h * PAIR, (h + 1) * PAIR)
+            if h == 1:
+                for late in pair:
+                    fill(late, FILL_PIECE)
+            for q in range(EXPERTS // 2):
+                for a in pair:
+                    for e in range(2 * q, 2 * q + 2):
+                        place(e, a)
+            for a in pair:
+                finish(a)

@@ -102,9 +102,14 @@ def tile_scatter_matmul_kernel(tc, base, x, w, b, offs, out):
             if h == 1:
                 for late in pair:
                     fill(late, FILL_PIECE)
-            for q in range(EXPERTS // 2):
+            if h == 0:
+                for q in range(EXPERTS // 2):
+                    for a in pair:
+                        for e in range(2 * q, 2 * q + 2):
+                            place(e, a)
+            else:
                 for a in pair:
-                    for e in range(2 * q, 2 * q + 2):
+                    for e in range(EXPERTS):
                         place(e, a)
             for a in pair:
                 finish(a)

@@ -92,10 +92,9 @@ def tile_scatter_matmul_kernel(tc, base, x, w, b, offs, out):
             bias_column = bias[:, a * BLOCK : a * BLOCK + 1]
             if a % 2 == 0:
                 nc.scalar.activation(result[:], windows[a][:], RELU, bias=bias_column)
-                nc.scalar.dma_start(out[a * P : (a + 1) * P, :], result[:])
             else:
                 nc.vector.tensor_scalar(result[:], windows[a][:], bias_column, 0.0, ADD, MAX)
-                nc.sync.dma_start(out[a * P : (a + 1) * P, :], result[:])
+            nc.sync.dma_start(out[a * P : (a + 1) * P, :], result[:])
 
         for h in range(WINDOWS // PAIR):
             pair = range(h * PAIR, (h + 1) * PAIR)

@@ -34,10 +34,6 @@ def tile_scatter_matmul_kernel(tc, base, x, w, b, offs, out):
 
         bias_rows = held.tile([P, P], F32, name="bias_rows", align_bytes=64)
         nc.gpsimd.memset(bias_rows[:], 0.0)
-        nc.scalar.dma_start(
-            bias_rows[0:P:BLOCK, :].rearrange("g (a i) -> g a i", i=BLOCK),
-            b.rearrange("(a g i) o -> g a (i o)", g=P // BLOCK, i=BLOCK),
-        )
 
         ident = held.tile([P, P], BF16, name="ident")
         make_identity(nc, ident[:])
@@ -50,9 +46,6 @@ def tile_scatter_matmul_kernel(tc, base, x, w, b, offs, out):
         nc.vector.memset(scratch[:], 0.0)
         nc.scalar.activation(scratch[:], scratch[:], RELU)
 
-        bias = held.tile([P, P], F32, name="bias", align_bytes=64)
-        nc.vector.transpose(bias[:], bias_rows[:])
-
         base_blocks = [held.tile([P, TOKENS], BF16, name="base%d" % a) for a in range(WINDOWS)]
         x_tile = held.tile([P, LISTED], BF16, name="x_tile")
         offsets = held.tile([P, LISTED // 16], U16, name="offsets")
@@ -62,11 +55,18 @@ def tile_scatter_matmul_kernel(tc, base, x, w, b, offs, out):
             for a in range(h * PAIR, (h + 1) * PAIR):
                 nc.sync.dma_start(base_blocks[a][:], base[a * P : (a + 1) * P, :])
             if h == 0:
+                nc.sync.dma_start(
+                    bias_rows[0:P:BLOCK, :].rearrange("g (a i) -> g a i", i=BLOCK),
+                    b.rearrange("(a g i) o -> g a (i o)", g=P // BLOCK, i=BLOCK),
+                )
                 nc.sync.dma_start(offsets[:], offs)
                 nc.sync.dma_start(x_tile[:], x)
             for q in range(EXPERTS // 2):
                 w_parts[h, q] = held.tile([P, 2, HALF], BF16, name="w_part%d_%d" % (h, q))
                 nc.sync.dma_start(w_parts[h, q][:], w_by_k[:, 2 * q : 2 * q + 2, h * HALF : (h + 1) * HALF])
+
+        bias = held.tile([P, P], F32, name="bias", align_bytes=64)
+        nc.vector.transpose(bias[:], bias_rows[:])
 
         windows = [banks.tile([P, TOKENS], F32, name="window%d" % a) for a in range(WINDOWS)]
 

@@ -55,15 +55,16 @@ def tile_scatter_matmul_kernel(tc, base, x, w, b, offs, out):
             for a in range(h * PAIR, (h + 1) * PAIR):
                 nc.sync.dma_start(base_blocks[a][:], base[a * P : (a + 1) * P, :])
             if h == 0:
-                nc.sync.dma_start(
-                    bias_rows[0:P:BLOCK, :].rearrange("g (a i) -> g a i", i=BLOCK),
-                    b.rearrange("(a g i) o -> g a (i o)", g=P // BLOCK, i=BLOCK),
-                )
                 nc.sync.dma_start(offsets[:], offs)
                 nc.sync.dma_start(x_tile[:], x)
             for q in range(EXPERTS // 2):
                 w_parts[h, q] = held.tile([P, 2, HALF], BF16, name="w_part%d_%d" % (h, q))
                 nc.sync.dma_start(w_parts[h, q][:], w_by_k[:, 2 * q : 2 * q + 2, h * HALF : (h + 1) * HALF])
+                if h == 0 and q == 0:
+                    nc.sync.dma_start(
+                        bias_rows[0:P:BLOCK, :].rearrange("g (a i) -> g a i", i=BLOCK),
+                        b.rearrange("(a g i) o -> g a (i o)", g=P // BLOCK, i=BLOCK),
+                    )
 
         bias = held.tile([P, P], F32, name="bias", align_bytes=64)
         nc.vector.transpose(bias[:], bias_rows[:])

@@ -92,9 +92,9 @@ def tile_scatter_matmul_kernel(tc, base, x, w, b, offs, out):
             result = held.tile([P, TOKENS], F32, name="result%d" % a)
             bias_column = bias[:, a * BLOCK : a * BLOCK + 1]
             if a % 2 == 0:
-                nc.scalar.activation(result[:], windows[a][:], RELU, bias=bias_column)
-            else:
                 nc.vector.tensor_scalar(result[:], windows[a][:], bias_column, 0.0, ADD, MAX)
+            else:
+                nc.scalar.activation(result[:], windows[a][:], RELU, bias=bias_column)
             nc.sync.dma_start(out[a * P : (a + 1) * P, :], result[:])
 
         for h in range(WINDOWS // PAIR):

@@ -19,6 +19,7 @@ FILL_PIECE = 44
 
 WARMUPS = 8
 BLOCK = 32
+DMA_ALIGN = 256
 
 FLOPS = 2 * P * FEATURES * LISTED
 
@@ -46,8 +47,10 @@ def tile_scatter_matmul_kernel(tc, base, x, w, b, offs, out):
         nc.vector.memset(scratch[:], 0.0)
         nc.scalar.activation(scratch[:], scratch[:], RELU)
 
-        base_blocks = [held.tile([P, TOKENS], BF16, name="base%d" % a) for a in range(WINDOWS)]
-        x_tile = held.tile([P, LISTED], BF16, name="x_tile")
+        base_blocks = [
+            held.tile([P, TOKENS], BF16, name="base%d" % a, align_bytes=DMA_ALIGN) for a in range(WINDOWS)
+        ]
+        x_tile = held.tile([P, LISTED], BF16, name="x_tile", align_bytes=DMA_ALIGN)
         offsets = held.tile([P, LISTED // 16], U16, name="offsets")
         w_by_k = w.rearrange("e k m -> k e m")
         w_parts = {}
@@ -58,7 +61,7 @@ def tile_scatter_matmul_kernel(tc, base, x, w, b, offs, out):
                 nc.sync.dma_start(offsets[:], offs)
                 nc.sync.dma_start(x_tile[:], x)
             for q in range(EXPERTS // 2):
-                w_parts[h, q] = held.tile([P, 2, HALF], BF16, name="w_part%d_%d" % (h, q))
+                w_parts[h, q] = held.tile([P, 2, HALF], BF16, name="w_part%d_%d" % (h, q), align_bytes=DMA_ALIGN)
                 nc.sync.dma_start(w_parts[h, q][:], w_by_k[:, 2 * q : 2 * q + 2, h * HALF : (h + 1) * HALF])
                 if h == 0 and q == 0:
                     nc.sync.dma_start(
@@ -89,7 +92,7 @@ def tile_scatter_matmul_kernel(tc, base, x, w, b, offs, out):
             )
 
         def finish(a):
-            result = held.tile([P, TOKENS], F32, name="result%d" % a)
+            result = held.tile([P, TOKENS], F32, name="result%d" % a, align_bytes=DMA_ALIGN)
             bias_column = bias[:, a * BLOCK : a * BLOCK + 1]
             if a % 2 == 0:
                 nc.vector.tensor_scalar(result[:], windows[a][:], bias_column, 0.0, ADD, MAX)

@@ -105,14 +105,8 @@ def tile_scatter_matmul_kernel(tc, base, x, w, b, offs, out):
             if h == 1:
                 for late in pair:
                     fill(late, FILL_PIECE)
-            if h == 0:
-                for q in range(EXPERTS // 2):
-                    for a in pair:
-                        for e in range(2 * q, 2 * q + 2):
-                            place(e, a)
-            else:
-                for a in pair:
-                    for e in range(EXPERTS):
-                        place(e, a)
+            for a in pair:
+                for e in range(EXPERTS):
+                    place(e, a)
             for a in pair:
                 finish(a)

@@ -17,7 +17,7 @@ HALF = FEATURES // 2
 PAIR = 2
 FILL_PIECE = 44
 
-WARMUPS = 8
+WARMUPS = 2
 BLOCK = 32
 DMA_ALIGN = 256
 
@@ -39,9 +39,12 @@ def tile_scatter_matmul_kernel(tc, base, x, w, b, offs, out):
         ident = held.tile([P, P], BF16, name="ident")
         make_identity(nc, ident[:])
 
-        unread = banks.tile([P, P], F32, name="unread")
+        repeats = TOKENS // P
+        unread = banks.tile([P, repeats, P], F32, name="unread")
         for _ in range(WARMUPS):
-            nc.tensor.matmul(unread[:], zeros[:], zeros[:], start=True, stop=True)
+            nc.tensor.matmul(
+                unread[:], zeros[:], zeros[:].unsqueeze(1).to_broadcast([P, repeats, P]), start=True, stop=True
+            )
 
         scratch = held.tile([P, 1], F32, name="scratch")
         nc.vector.memset(scratch[:], 0.0)

@@ -15,7 +15,8 @@ PIECE_COLS = PIECE // 16
 WINDOWS = FEATURES // P
 HALF = FEATURES // 2
 PAIR = 2
-FILL_PIECE = 44
+STRIP = 32
+FILL_PIECE = 172
 
 WARMUPS = 2
 BLOCK = 32
@@ -77,13 +78,20 @@ def tile_scatter_matmul_kernel(tc, base, x, w, b, offs, out):
 
         windows = [banks.tile([P, TOKENS], F32, name="window%d" % a) for a in range(WINDOWS)]
 
-        def fill(a, piece):
-            for c in range(0, TOKENS, piece):
-                end = min(c + piece, TOKENS)
-                nc.tensor.matmul(windows[a][:, c:end], ident[:], base_blocks[a][:, c:end], start=True, stop=True)
-
         for a in range(PAIR):
-            fill(a, TOKENS)
+            nc.tensor.matmul(windows[a][:], ident[:], base_blocks[a][:], start=True, stop=True)
+
+        def fill_by_strips(a):
+            for c in range(0, TOKENS, FILL_PIECE):
+                end = min(c + FILL_PIECE, TOKENS)
+                for j in range(0, P, STRIP):
+                    nc.tensor.matmul(
+                        windows[a][j : j + STRIP, c:end],
+                        ident[:, j : j + STRIP],
+                        base_blocks[a][:, c:end],
+                        start=True,
+                        stop=True,
+                    )
 
         def place(e, a):
             nc.tensor.matmul(
@@ -107,7 +115,7 @@ def tile_scatter_matmul_kernel(tc, base, x, w, b, offs, out):
             pair = range(h * PAIR, (h + 1) * PAIR)
             if h == 1:
                 for late in pair:
-                    fill(late, FILL_PIECE)
+                    fill_by_strips(late)
             for a in pair:
                 for e in range(EXPERTS):
                     place(e, a)

import concourse.mybir as mybir
from concourse.masks import make_identity

BF16, F32, U16 = mybir.dt.bfloat16, mybir.dt.float32, mybir.dt.uint16
ADD, MAX = mybir.AluOpType.add, mybir.AluOpType.max
RELU = mybir.ActivationFunctionType.Relu

P = 128
TOKENS = 512
FEATURES = 512
LISTED = 256
EXPERTS = 4
PIECE = LISTED // EXPERTS
PIECE_COLS = PIECE // 16
WINDOWS = FEATURES // P
HALF = FEATURES // 2
PAIR = 2
STRIP = 32
FILL_PIECE = 172

WARMUPS = 2
BLOCK = 32
DMA_ALIGN = 256

FLOPS = 2 * P * FEATURES * LISTED


def tile_scatter_matmul_kernel(tc, base, x, w, b, offs, out):
    nc = tc.nc
    with (
        tc.tile_pool(name="held", bufs=1) as held,
        tc.psum_pool(name="banks", bufs=1) as banks,
    ):
        zeros = held.tile([P, P], BF16, name="zeros")
        nc.vector.memset(zeros[:], 0.0)

        bias_rows = held.tile([P, P], F32, name="bias_rows", align_bytes=64)
        nc.gpsimd.memset(bias_rows[:], 0.0)

        ident = held.tile([P, P], BF16, name="ident")
        make_identity(nc, ident[:])

        repeats = TOKENS // P
        unread = banks.tile([P, repeats, P], F32, name="unread")
        for _ in range(WARMUPS):
            nc.tensor.matmul(
                unread[:], zeros[:], zeros[:].unsqueeze(1).to_broadcast([P, repeats, P]), start=True, stop=True
            )

        scratch = held.tile([P, 1], F32, name="scratch")
        nc.vector.memset(scratch[:], 0.0)
        nc.scalar.activation(scratch[:], scratch[:], RELU)

        base_blocks = [
            held.tile([P, TOKENS], BF16, name="base%d" % a, align_bytes=DMA_ALIGN) for a in range(WINDOWS)
        ]
        x_tile = held.tile([P, LISTED], BF16, name="x_tile", align_bytes=DMA_ALIGN)
        offsets = held.tile([P, LISTED // 16], U16, name="offsets")
        w_by_k = w.rearrange("e k m -> k e m")
        w_parts = {}
        for h in range(WINDOWS // PAIR):
            for a in range(h * PAIR, (h + 1) * PAIR):
                nc.sync.dma_start(base_blocks[a][:], base[a * P : (a + 1) * P, :])
            if h == 0:
                nc.sync.dma_start(offsets[:], offs)
                nc.sync.dma_start(x_tile[:], x)
            for q in range(EXPERTS // 2):
                w_parts[h, q] = held.tile([P, 2, HALF], BF16, name="w_part%d_%d" % (h, q), align_bytes=DMA_ALIGN)
                nc.sync.dma_start(w_parts[h, q][:], w_by_k[:, 2 * q : 2 * q + 2, h * HALF : (h + 1) * HALF])
                if h == 0 and q == 0:
                    nc.sync.dma_start(
                        bias_rows[0:P:BLOCK, :].rearrange("g (a i) -> g a i", i=BLOCK),
                        b.rearrange("(a g i) o -> g a (i o)", g=P // BLOCK, i=BLOCK),
                    )

        bias = held.tile([P, P], F32, name="bias", align_bytes=64)
        nc.vector.transpose(bias[:], bias_rows[:])

        windows = [banks.tile([P, TOKENS], F32, name="window%d" % a) for a in range(WINDOWS)]

        for a in range(PAIR):
            nc.tensor.matmul(windows[a][:], ident[:], base_blocks[a][:], start=True, stop=True)

        def fill_by_strips(a):
            for c in range(0, TOKENS, FILL_PIECE):
                end = min(c + FILL_PIECE, TOKENS)
                for j in range(0, P, STRIP):
                    nc.tensor.matmul(
                        windows[a][j : j + STRIP, c:end],
                        ident[:, j : j + STRIP],
                        base_blocks[a][:, c:end],
                        start=True,
                        stop=True,
                    )

        def place(e, a):
            nc.tensor.matmul(
                windows[a][:].indirect(offsets[:, e * PIECE_COLS : (e + 1) * PIECE_COLS]),
                w_parts[a // 2, e // 2][:, e % 2, (a % 2) * P : (a % 2 + 1) * P],
                x_tile[:, e * PIECE : (e + 1) * PIECE],
                start=True,
                stop=True,
            )

        def finish(a):
            result = held.tile([P, TOKENS], F32, name="result%d" % a, align_bytes=DMA_ALIGN)
            bias_column = bias[:, a * BLOCK : a * BLOCK + 1]
            if a % 2 == 0:
                nc.vector.tensor_scalar(result[:], windows[a][:], bias_column, 0.0, ADD, MAX)
            else:
                nc.scalar.activation(result[:], windows[a][:], RELU, bias=bias_column)
            nc.sync.dma_start(out[a * P : (a + 1) * P, :], result[:])

        for h in range(WINDOWS // PAIR):
            pair = range(h * PAIR, (h + 1) * PAIR)
            if h == 1:
                for late in pair:
                    fill_by_strips(late)
            for a in pair:
                for e in range(EXPERTS):
                    place(e, a)
            for a in pair:
                finish(a)
